import numpy as np
CORES = [0,1,2,3,4,5,6,7,8,9,10,11,12,13,14,15,16,17,18,19,20,21,22,23,24,25,26,27,28,29,30,31,32,33,34,35,36,37,38,39,40,41,42,43,44,45,46,47,48,49,50,51,52,53,54,55,56,57,58,59,60,61,62,63,64,65,66,67,68,69,70,71,72,73,74,75,76,77,78,79,80,81,82,83,84,85,86,87,88,89,90,91,92,93,94,95,96,97,98,99,100,101,102,103,104,105,106,107,108,109,110,111,112,113,114,115,116,117,118,119,120,121,122,123,124,125,126,127,128,129,130,131,132,133,134,135,136,137,138,139,140,141,142,143,144,145,146,147,148,149,150,151,152,153,154,155,156,157,158,159,160,161,162,163,164,165,166,167,168,169,170,171,172,173,174,175,176,177,178,179,180,181,182,183,184,185,186,187,188,189,190,191,192,193,194,195,196,197,198,199,200,201,202,203,204,205,206,207,208,209,210,211,212,213,214,215,216,217,218,219,220,221,222,223,224,225,226,227,228,229,230,231,232,233,234,235,236,237,238,239,240,241,242,243,244,245,246,247,248,249,250,251,252,253,254,255,256,257,258,259,260,261,262,263,264,265,266,267,268,269,270,271,272,273,274,275,276,277,278,279,280,281,282,283,284,285,286,287,288,289,290,291,292,293,294,295,296,297,298,299,300,301,302,303,304,305,306,307,308,309,310,311,312,313,314,315,316,317,318,319,320,321,322,323,324,325,326,327,328,329,330,331,332,333,334,335,336,337,338,339,340,341,342,343,344,345,346,347,348,349,350,351,352,353,354,355,356,357,358,359,360,361,362,363,364,365,366,367,368,369,370,371,372,373,374,375,376,377,378,379,380,381,382,383,384,385,386,387,388,389,390,391,392,393,394,395,396,397,398,399,400,401,402,403,404,405,406,407,408,409,410,411,412,413,414,415,416,417,418,419,420,421,422,423,424,425,426,427,428,429,430,431,432,433,434,435,436,437,438,439,440,441,442,443,444,445,446,447,448,449,450,451,452,453,454,455,456,457,458,459,460,461,462,463,464,465,466,467,468,469,470,471,472,473,474,475,476,477,478,479,480,481,482,483,484,485,486,487,488,489,490,491,492,493,494,495,496,497,498,499,500,501,502,503,504,505,506,507,508,509,510,511]
N = 512
def setup_inputs(rng):
    return {"x": rng.standard_normal((N, 128, 4), dtype=np.float32)}
def reference(x):
    g = np.concatenate(list(x), axis=1)
    return {"y": np.broadcast_to(g, (N,) + g.shape)}

@@ -1,0 +1,191 @@
+import concourse.bass as bass
+
+COLS = 4
+UNIT = 8
+RANGE = 128
+S_OF = {"dg": 2, "own": 3, "nb": 6, "cab": 7}
+R_OF = {"dg": 0, "own": 4, "nb": 1, "cab": 5}
+ROLES = ("own", "nb", "cab", "dg")
+ROUNDS = 4
+
+SCRATCH = {
+    "full": ("sbuf", [128, 512 * COLS], "float32"),
+}
+SEMAPHORES = ["loaded", "sent", "a1", "a2", "a3", "a4", "stored"]
+
+PLAN = {}
+
+
+def host_of(h, role):
+    return {"own": h, "nb": h ^ 1, "cab": 3 - h, "dg": h ^ 2}[role]
+
+
+def cid(h, k, i):
+    return h * 128 + k * 8 + i
+
+
+def enters_at_s(k, role, u):
+    if role == "dg":
+        return u == k
+    return (u & 1) == (k & 1)
+
+
+def split(k, role):
+    if role == "own":
+        s0, r0 = 9 + 64 + 32, 9 + 24
+    elif role == "nb":
+        s0, r0 = 9 + 64 + 56, 9
+    elif role == "cab":
+        s0, r0 = 9 + 64 + 64, 9
+    else:
+        s0, r0 = 9 + 120, 9
+    best = None
+    for t in range(17):
+        for low in (True, False):
+            s, r = s0, r0
+            for u in range(16):
+                if role == "own" and u == k:
+                    continue
+                if (u < t) == low:
+                    s += 7 * UNIT
+                elif enters_at_s(k, role, u):
+                    s += UNIT
+                    r += 6 * UNIT
+                else:
+                    r += 7 * UNIT
+            key = (max(s, r), 0 if low else 1, t)
+            if best is None or key < best[0]:
+                best = (key, [(u < t) == low for u in range(16)])
+    return best[1]
+
+
+def runs(blocks):
+    out = []
+    for b in blocks:
+        if out and out[-1][0] + out[-1][1] == b:
+            out[-1][1] += 1
+        else:
+            out.append([b, 1])
+    return out
+
+
+def build_writes():
+    owner, entry = {}, {}
+    for h in range(4):
+        for k in range(16):
+            ow, en = [None] * 64, [None] * 64
+            for role in ROLES:
+                mine = split(k, role)
+                for u in range(16):
+                    if role == "own" and u == k:
+                        continue
+                    o = S_OF[role] if mine[u] else R_OF[role]
+                    ow[host_of(h, role) * 16 + u] = o
+                    en[host_of(h, role) * 16 + u] = S_OF[role] if enters_at_s(k, role, u) else o
+            owner[(h, k)], entry[(h, k)] = ow, en
+
+    writes = [{} for d in range(ROUNDS + 1)]
+
+    def add(d, src, dst, lo, n):
+        writes[d].setdefault(src, {}).setdefault((lo, n), []).append(dst)
+
+    for h in range(4):
+        for k in range(16):
+            ow, en = owner[(h, k)], entry[(h, k)]
+            for i in range(8):
+                c = cid(h, k, i)
+                for j in range(8):
+                    if j != i:
+                        add(1, c, cid(h, k, j), c, 1)
+                add(1, c, cid(h ^ 1, k, S_OF["nb"]), c, 1)
+                add(1, c, cid(3 - h, k, S_OF["cab"]), c, 1)
+            for role in ("own", "nb", "cab"):
+                lo = (host_of(h, role) * 16 + k) * UNIT
+                for step in range(1, 8):
+                    k2 = (k + 2 * step) % 16
+                    src = R_OF[role] if role == "own" and step > 4 else S_OF[role]
+                    add(2, cid(h, k, src), cid(h, k2, S_OF[role]), lo, UNIT)
+                if role == "cab":
+                    add(2, cid(h, k, S_OF[role]), cid(h ^ 1, k, S_OF["dg"]), lo, UNIT)
+            for role in ("own", "nb", "cab"):
+                src = S_OF[role]
+                for u in range(k & 1, 16, 2):
+                    v = host_of(h, role) * 16 + u
+                    add(3, cid(h, k, src), cid(h, k ^ 1, entry[(h, k ^ 1)][v]), v * UNIT, UNIT)
+                    if ow[v] is not None and ow[v] != src:
+                        add(3, cid(h, k, src), cid(h, k, ow[v]), v * UNIT, UNIT)
+            src = S_OF["dg"]
+            v = host_of(h, "dg") * 16 + k
+            for k2 in range(16):
+                if k2 != k:
+                    add(3, cid(h, k, src), cid(h, k2, entry[(h, k2)][v]), v * UNIT, UNIT)
+            if ow[v] != src:
+                add(3, cid(h, k, src), cid(h, k, ow[v]), v * UNIT, UNIT)
+            for o in range(8):
+                for t in range(8):
+                    if t != o:
+                        for lo, n in runs([v for v in range(64) if ow[v] == o and en[v] != t]):
+                            add(4, cid(h, k, o), cid(h, k, t), lo * UNIT, n * UNIT)
+    return writes
+
+
+def plan():
+    if PLAN:
+        return PLAN["calls"], PLAN["expect"], PLAN["sent"]
+    writes = build_writes()
+    calls = [[[] for d in range(ROUNDS + 1)] for c in range(512)]
+    expect = [[0] * (ROUNDS + 1) for c in range(512)]
+    sent = [0] * 512
+    for d in range(1, ROUNDS + 1):
+        for src, trs in writes[d].items():
+            widths = {}
+            for (lo, n), dsts in sorted(trs.items()):
+                widths.setdefault(n, []).append((lo, n, dsts))
+            for n in sorted(widths):
+                group = widths[n]
+                on_chip = all(t // 8 == src // 8 for tr in group for t in tr[2])
+                cap = 16 if on_chip else 8
+                for first in range(0, len(group), cap):
+                    part = group[first:first + cap]
+                    e = 1
+                    while 2 * e * len(part) <= cap:
+                        e *= 2
+                    call = []
+                    for i, (lo, m, dsts) in enumerate(part):
+                        call.append((lo, m, dsts, ((1 << e) - 1) << (i * e)))
+                        sent[src] += e
+                        for t in dsts:
+                            expect[t][d] += e
+                    calls[src][d].append(call)
+    PLAN["calls"], PLAN["expect"], PLAN["sent"] = calls, expect, sent
+    return calls, expect, sent
+
+
+def rank_program(g, core, T, topo):
+    if T.rank_of(core) is None:
+        return
+    calls, expect, sent = plan()
+    full = T.full
+    arrived = [None, T.sem.a1, T.sem.a2, T.sem.a3, T.sem.a4]
+
+    g.dma_start(full[:, core * COLS:(core + 1) * COLS], T.x[:]).then_inc(T.sem.loaded, 16)
+    g.wait_ge(T.sem.loaded, 16)
+
+    for d in range(1, ROUNDS + 1):
+        for call in calls[core][d]:
+            transfers = []
+            for lo, n, dsts, mask in call:
+                piece = full[:, lo * COLS:(lo + n) * COLS]
+                ids = []
+                for t in dsts:
+                    rid, pid = topo.addr(t, core)
+                    ids.append(bass.DstId(rid=rid, pnc=pid))
+                transfers.append(bass.RemoteDMATransfer(dst_ids=ids, dma_engine_mask=mask, remote_sem=arrived[d],
+                                                        srcs=[piece], dsts=[piece for t in dsts]))
+            g.remote_dma_fused(transfers, local_sem=T.sem.sent)
+        if expect[core][d]:
+            g.wait_ge(arrived[d], expect[core][d])
+
+    g.wait_ge(T.sem.sent, sent[core])
+    g.dma_start(T.y[:], full[:]).then_inc(T.sem.stored, 16)
+    g.wait_ge(T.sem.stored, 16)

@@ -3,10 +3,9 @@ import concourse.bass as bass
 COLS = 4
 UNIT = 8
 RANGE = 128
-S_OF = {"dg": 2, "own": 3, "nb": 6, "cab": 7}
-R_OF = {"dg": 0, "own": 4, "nb": 1, "cab": 5}
-ROLES = ("own", "nb", "cab", "dg")
 ROUNDS = 4
+ROLES = ("own", "nb", "cab", "dg")
+BASE = {"s_dg": 2, "s_nb": 3, "r_nb": 0, "r_own": 1, "s_own": 6, "s_cab": 7, "r_cab": 4, "r_dg": 5}
 
 SCRATCH = {
     "full": ("sbuf", [128, 512 * COLS], "float32"),
@@ -24,108 +23,102 @@ def cid(h, k, i):
     return h * 128 + k * 8 + i
 
 
-def enters_at_s(k, role, u):
-    if role == "dg":
-        return u == k
-    return (u & 1) == (k & 1)
+def core_of(k, name):
+    return BASE[name] ^ (4 if k & 1 else 0)
 
 
-def split(k, role):
+def s_part(k, role):
+    if role in ("nb", "cab"):
+        return (68, 60) if k < 8 else (0, 60)
     if role == "own":
-        s0, r0 = 9 + 64 + 32, 9 + 24
-    elif role == "nb":
-        s0, r0 = 9 + 64 + 56, 9
-    elif role == "cab":
-        s0, r0 = 9 + 64 + 64, 9
-    else:
-        s0, r0 = 9 + 120, 9
-    best = None
-    for t in range(17):
-        for low in (True, False):
-            s, r = s0, r0
-            for u in range(16):
-                if role == "own" and u == k:
-                    continue
-                if (u < t) == low:
-                    s += 7 * UNIT
-                elif enters_at_s(k, role, u):
-                    s += UNIT
-                    r += 6 * UNIT
-                else:
-                    r += 7 * UNIT
-            key = (max(s, r), 0 if low else 1, t)
-            if best is None or key < best[0]:
-                best = (key, [(u < t) == low for u in range(16)])
-    return best[1]
+        if k == 7:
+            return (0, 56)
+        if k == 8:
+            return (72, 56)
+        return (80, 48) if k < 8 else (0, 48)
+    first = 0 if k < 7 else 9 if k > 8 else 1 if k == 7 else 8
+    return (first * UNIT, 7 * UNIT)
 
 
-def runs(blocks):
+def runs(items):
     out = []
-    for b in blocks:
-        if out and out[-1][0] + out[-1][1] == b:
+    for b, key in items:
+        if out and out[-1][2] == key and out[-1][0] + out[-1][1] == b:
             out[-1][1] += 1
         else:
-            out.append([b, 1])
+            out.append([b, 1, key])
     return out
 
 
+def chip_tables(h, k):
+    owner, early = [None] * 512, [()] * 512
+    for role in ROLES:
+        s, r = core_of(k, "s_" + role), core_of(k, "r_" + role)
+        first, count = s_part(k, role)
+        for b in range(RANGE):
+            u = b // UNIT
+            if role == "own" and u == k:
+                continue
+            j = host_of(h, role) * RANGE + b
+            owner[j] = s if first <= b < first + count else r
+            if role == "dg":
+                early[j] = (s,) if u == k else ()
+            elif u == k:
+                early[j] = (s, r)
+            elif (u & 1) == (k & 1):
+                early[j] = (s,)
+    return owner, early
+
+
 def build_writes():
-    owner, entry = {}, {}
+    tables = {}
     for h in range(4):
         for k in range(16):
-            ow, en = [None] * 64, [None] * 64
-            for role in ROLES:
-                mine = split(k, role)
-                for u in range(16):
-                    if role == "own" and u == k:
-                        continue
-                    o = S_OF[role] if mine[u] else R_OF[role]
-                    ow[host_of(h, role) * 16 + u] = o
-                    en[host_of(h, role) * 16 + u] = S_OF[role] if enters_at_s(k, role, u) else o
-            owner[(h, k)], entry[(h, k)] = ow, en
-
+            tables[(h, k)] = chip_tables(h, k)
     writes = [{} for d in range(ROUNDS + 1)]
 
     def add(d, src, dst, lo, n):
         writes[d].setdefault(src, {}).setdefault((lo, n), []).append(dst)
 
+    def spread(h, k, src, lo, chips):
+        for k2 in chips:
+            there = tables[(h, k2)][0]
+            for first, n, o in runs([(b, there[b]) for b in range(lo, lo + UNIT)]):
+                add(3, cid(h, k, src), cid(h, k2, o), first, n)
+        owner, early = tables[(h, k)]
+        for first, n, o in runs([(b, owner[b]) for b in range(lo, lo + UNIT)
+                                 if owner[b] is not None and owner[b] not in early[b]]):
+            add(3, cid(h, k, src), cid(h, k, o), first, n)
+
     for h in range(4):
         for k in range(16):
-            ow, en = owner[(h, k)], entry[(h, k)]
+            owner, early = tables[(h, k)]
             for i in range(8):
                 c = cid(h, k, i)
                 for j in range(8):
                     if j != i:
                         add(1, c, cid(h, k, j), c, 1)
-                add(1, c, cid(h ^ 1, k, S_OF["nb"]), c, 1)
-                add(1, c, cid(3 - h, k, S_OF["cab"]), c, 1)
+                add(1, c, cid(h ^ 1, k, core_of(k, "r_nb")), c, 1)
+                add(1, c, cid(3 - h, k, core_of(k, "r_cab")), c, 1)
             for role in ("own", "nb", "cab"):
-                lo = (host_of(h, role) * 16 + k) * UNIT
+                lo = host_of(h, role) * RANGE + k * UNIT
+                s, r = core_of(k, "s_" + role), core_of(k, "r_" + role)
                 for step in range(1, 8):
-                    k2 = (k + 2 * step) % 16
-                    src = R_OF[role] if role == "own" and step > 4 else S_OF[role]
-                    add(2, cid(h, k, src), cid(h, k2, S_OF[role]), lo, UNIT)
+                    src = s if role == "own" and step > 4 else r
+                    add(2, cid(h, k, src), cid(h, (k + 2 * step) % 16, s), lo, UNIT)
+                if role != "own":
+                    add(2, cid(h, k, r), cid(h, k, s), lo, UNIT)
                 if role == "cab":
-                    add(2, cid(h, k, S_OF[role]), cid(h ^ 1, k, S_OF["dg"]), lo, UNIT)
+                    add(2, cid(h, k, r), cid(h ^ 1, k, core_of(k, "s_dg")), lo, UNIT)
             for role in ("own", "nb", "cab"):
-                src = S_OF[role]
                 for u in range(k & 1, 16, 2):
-                    v = host_of(h, role) * 16 + u
-                    add(3, cid(h, k, src), cid(h, k ^ 1, entry[(h, k ^ 1)][v]), v * UNIT, UNIT)
-                    if ow[v] is not None and ow[v] != src:
-                        add(3, cid(h, k, src), cid(h, k, ow[v]), v * UNIT, UNIT)
-            src = S_OF["dg"]
-            v = host_of(h, "dg") * 16 + k
-            for k2 in range(16):
-                if k2 != k:
-                    add(3, cid(h, k, src), cid(h, k2, entry[(h, k2)][v]), v * UNIT, UNIT)
-            if ow[v] != src:
-                add(3, cid(h, k, src), cid(h, k, ow[v]), v * UNIT, UNIT)
+                    spread(h, k, core_of(k, "s_" + role), host_of(h, role) * RANGE + u * UNIT, [k ^ 1])
+            spread(h, k, core_of(k, "s_dg"), host_of(h, "dg") * RANGE + k * UNIT, [k2 for k2 in range(16) if k2 != k])
             for o in range(8):
                 for t in range(8):
                     if t != o:
-                        for lo, n in runs([v for v in range(64) if ow[v] == o and en[v] != t]):
-                            add(4, cid(h, k, o), cid(h, k, t), lo * UNIT, n * UNIT)
+                        for first, n, key in runs([(b, 0) for b in range(512) if owner[b] == o and t not in early[b]]):
+                            add(4, cid(h, k, o), cid(h, k, t), first, n)
     return writes
 
 

@@ -35,7 +35,7 @@ def s_part(k, role):
             return (0, 56)
         if k == 8:
             return (72, 56)
-        return (80, 48) if k < 8 else (0, 48)
+        return (80, 48) if k < 6 or k == 9 else (0, 48)
     first = 0 if k < 7 else 9 if k > 8 else 1 if k == 7 else 8
     return (first * UNIT, 7 * UNIT)
 

import concourse.bass as bass

COLS = 4
UNIT = 8
RANGE = 128
ROUNDS = 4
ROLES = ("own", "nb", "cab", "dg")
BASE = {"s_dg": 2, "s_nb": 3, "r_nb": 0, "r_own": 1, "s_own": 6, "s_cab": 7, "r_cab": 4, "r_dg": 5}

SCRATCH = {
    "full": ("sbuf", [128, 512 * COLS], "float32"),
}
SEMAPHORES = ["loaded", "sent", "a1", "a2", "a3", "a4", "stored"]

PLAN = {}


def host_of(h, role):
    return {"own": h, "nb": h ^ 1, "cab": 3 - h, "dg": h ^ 2}[role]


def cid(h, k, i):
    return h * 128 + k * 8 + i


def core_of(k, name):
    return BASE[name] ^ (4 if k & 1 else 0)


def s_part(k, role):
    if role in ("nb", "cab"):
        return (68, 60) if k < 8 else (0, 60)
    if role == "own":
        if k == 7:
            return (0, 56)
        if k == 8:
            return (72, 56)
        return (80, 48) if k < 6 or k == 9 else (0, 48)
    first = 0 if k < 7 else 9 if k > 8 else 1 if k == 7 else 8
    return (first * UNIT, 7 * UNIT)


def runs(items):
    out = []
    for b, key in items:
        if out and out[-1][2] == key and out[-1][0] + out[-1][1] == b:
            out[-1][1] += 1
        else:
            out.append([b, 1, key])
    return out


def chip_tables(h, k):
    owner, early = [None] * 512, [()] * 512
    for role in ROLES:
        s, r = core_of(k, "s_" + role), core_of(k, "r_" + role)
        first, count = s_part(k, role)
        for b in range(RANGE):
            u = b // UNIT
            if role == "own" and u == k:
                continue
            j = host_of(h, role) * RANGE + b
            owner[j] = s if first <= b < first + count else r
            if role == "dg":
                early[j] = (s,) if u == k else ()
            elif u == k:
                early[j] = (s, r)
            elif (u & 1) == (k & 1):
                early[j] = (s,)
    return owner, early


def build_writes():
    tables = {}
    for h in range(4):
        for k in range(16):
            tables[(h, k)] = chip_tables(h, k)
    writes = [{} for d in range(ROUNDS + 1)]

    def add(d, src, dst, lo, n):
        writes[d].setdefault(src, {}).setdefault((lo, n), []).append(dst)

    def spread(h, k, src, lo, chips):
        for k2 in chips:
            there = tables[(h, k2)][0]
            for first, n, o in runs([(b, there[b]) for b in range(lo, lo + UNIT)]):
                add(3, cid(h, k, src), cid(h, k2, o), first, n)
        owner, early = tables[(h, k)]
        for first, n, o in runs([(b, owner[b]) for b in range(lo, lo + UNIT)
                                 if owner[b] is not None and owner[b] not in early[b]]):
            add(3, cid(h, k, src), cid(h, k, o), first, n)

    for h in range(4):
        for k in range(16):
            owner, early = tables[(h, k)]
            for i in range(8):
                c = cid(h, k, i)
                for j in range(8):
                    if j != i:
                        add(1, c, cid(h, k, j), c, 1)
                add(1, c, cid(h ^ 1, k, core_of(k, "r_nb")), c, 1)
                add(1, c, cid(3 - h, k, core_of(k, "r_cab")), c, 1)
            for role in ("own", "nb", "cab"):
                lo = host_of(h, role) * RANGE + k * UNIT
                s, r = core_of(k, "s_" + role), core_of(k, "r_" + role)
                for step in range(1, 8):
                    src = s if role == "own" and step > 4 else r
                    add(2, cid(h, k, src), cid(h, (k + 2 * step) % 16, s), lo, UNIT)
                if role != "own":
                    add(2, cid(h, k, r), cid(h, k, s), lo, UNIT)
                if role == "cab":
                    add(2, cid(h, k, r), cid(h ^ 1, k, core_of(k, "s_dg")), lo, UNIT)
            for role in ("own", "nb", "cab"):
                for u in range(k & 1, 16, 2):
                    spread(h, k, core_of(k, "s_" + role), host_of(h, role) * RANGE + u * UNIT, [k ^ 1])
            spread(h, k, core_of(k, "s_dg"), host_of(h, "dg") * RANGE + k * UNIT, [k2 for k2 in range(16) if k2 != k])
            for o in range(8):
                for t in range(8):
                    if t != o:
                        for first, n, key in runs([(b, 0) for b in range(512) if owner[b] == o and t not in early[b]]):
                            add(4, cid(h, k, o), cid(h, k, t), first, n)
    return writes


def plan():
    if PLAN:
        return PLAN["calls"], PLAN["expect"], PLAN["sent"]
    writes = build_writes()
    calls = [[[] for d in range(ROUNDS + 1)] for c in range(512)]
    expect = [[0] * (ROUNDS + 1) for c in range(512)]
    sent = [0] * 512
    for d in range(1, ROUNDS + 1):
        for src, trs in writes[d].items():
            widths = {}
            for (lo, n), dsts in sorted(trs.items()):
                widths.setdefault(n, []).append((lo, n, dsts))
            for n in sorted(widths):
                group = widths[n]
                on_chip = all(t // 8 == src // 8 for tr in group for t in tr[2])
                cap = 16 if on_chip else 8
                for first in range(0, len(group), cap):
                    part = group[first:first + cap]
                    e = 1
                    while 2 * e * len(part) <= cap:
                        e *= 2
                    call = []
                    for i, (lo, m, dsts) in enumerate(part):
                        call.append((lo, m, dsts, ((1 << e) - 1) << (i * e)))
                        sent[src] += e
                        for t in dsts:
                            expect[t][d] += e
                    calls[src][d].append(call)
    PLAN["calls"], PLAN["expect"], PLAN["sent"] = calls, expect, sent
    return calls, expect, sent


def rank_program(g, core, T, topo):
    if T.rank_of(core) is None:
        return
    calls, expect, sent = plan()
    full = T.full
    arrived = [None, T.sem.a1, T.sem.a2, T.sem.a3, T.sem.a4]

    g.dma_start(full[:, core * COLS:(core + 1) * COLS], T.x[:]).then_inc(T.sem.loaded, 16)
    g.wait_ge(T.sem.loaded, 16)

    for d in range(1, ROUNDS + 1):
        for call in calls[core][d]:
            transfers = []
            for lo, n, dsts, mask in call:
                piece = full[:, lo * COLS:(lo + n) * COLS]
                ids = []
                for t in dsts:
                    rid, pid = topo.addr(t, core)
                    ids.append(bass.DstId(rid=rid, pnc=pid))
                transfers.append(bass.RemoteDMATransfer(dst_ids=ids, dma_engine_mask=mask, remote_sem=arrived[d],
                                                        srcs=[piece], dsts=[piece for t in dsts]))
            g.remote_dma_fused(transfers, local_sem=T.sem.sent)
        if expect[core][d]:
            g.wait_ge(arrived[d], expect[core][d])

    g.wait_ge(T.sem.sent, sent[core])
    g.dma_start(T.y[:], full[:]).then_inc(T.sem.stored, 16)
    g.wait_ge(T.sem.stored, 16)
